import numpy as np
import ml_dtypes


def mxq(x, axis, fmt="e4m3"):
    dtype, down = {"e4m3": (ml_dtypes.float8_e4m3fn, 7), "e5m2": (ml_dtypes.float8_e5m2, 14)}[fmt]
    v = np.moveaxis(np.asarray(x, np.float32).astype(ml_dtypes.bfloat16).astype(np.float64), axis, -1)
    blocks = v.reshape(v.shape[:-1] + (-1, 32))
    amax = np.abs(blocks).max(-1, keepdims=True)
    byte = np.maximum(np.where(amax > 0, np.frexp(amax)[1] - 1 + 127, 0) - down, 1)
    scale = np.exp2(byte - 127.0)
    codes = (blocks / scale).astype(np.float32).astype(dtype).astype(np.float64)
    return np.moveaxis((codes * scale).reshape(v.shape), -1, axis)


WIDE = False


def mx_kscale(k):
    if not WIDE:
        return np.ones(k)
    levels = np.array([30, -30])
    if k % 512:
        return np.exp2(np.random.permutation(np.resize(levels, k // 32))).repeat(32)
    a = np.empty((k // 512, 16))
    for p in range(k // 512):
        a[p, :8] = np.random.permutation(np.resize(levels, 8))
        for g in range(8):
            far = levels[np.abs(levels - a[p, g]) >= 10]
            a[p, g + 8] = far[np.random.randint(len(far))]
    return np.exp2(a.ravel()).repeat(32)


def f64(x):
    return np.asarray(x).astype(np.float64)


def striped(idx):
    return np.tile(np.asarray(idx).reshape(-1, 16).T, (8, 1)).astype(np.uint16)


def unstriped(offs):
    return offs[:16].T.reshape(-1).astype(np.int64)


E2M1 = np.array([0.0, 0.5, 1.0, 1.5, 2.0, 3.0, 4.0, 6.0, -0.0, -0.5, -1.0, -1.5, -2.0, -3.0, -4.0, -6.0])


def pack_weight(w, fmt):
    k, n = w.shape
    w = f64(np.asarray(w, np.float32).astype(ml_dtypes.bfloat16)).reshape(k // 32, 32, n)
    amax = np.abs(w).max(1)
    if fmt in ("e4m3", "e5m2"):
        byte = np.frexp(amax)[1] - 1 + 127 - (7 if fmt == "e4m3" else 14)
    else:
        mant, ex = np.frexp(amax / 6.0)
        byte = np.where(mant > 0.5, ex, ex - 1) + 127
    byte = np.clip(np.where(amax > 0, byte, 1), 1, 254)
    scaled = (w * np.exp2(127.0 - byte)[:, None, :]).reshape(k, n).astype(np.float32)
    by_word = np.ascontiguousarray(scaled.reshape(k // 512, 128, 4, n).transpose(0, 1, 3, 2))
    if fmt in ("e4m3", "e5m2"):
        words = by_word.astype(ml_dtypes.float8_e4m3fn if fmt == "e4m3" else ml_dtypes.float8_e5m2).view(np.uint8)
    else:
        c = by_word.astype(ml_dtypes.float4_e2m1fn).view(np.uint8) & 0xF
        words = (c[..., 0::2] | (c[..., 1::2] << 4)).reshape(k // 512, 128, 2 * n)
    return np.ascontiguousarray(words), np.ascontiguousarray(byte.astype(np.uint8).reshape(k // 512, 16, n))


def unpack_weight(words, scales, fmt):
    g, _, n = scales.shape
    words = np.ascontiguousarray(words).reshape(g, 128, n, -1)
    if fmt in ("e4m3", "e5m2"):
        vals = words.view(ml_dtypes.float8_e4m3fn if fmt == "e4m3" else ml_dtypes.float8_e5m2).astype(np.float64)
    else:
        nib = np.empty((g, 128, n, 4), np.uint8)
        nib[..., 0::2] = words & 0xF
        nib[..., 1::2] = words >> 4
        vals = E2M1[nib]
    vals = vals * np.repeat(np.exp2(scales.astype(np.float64) - 127.0), 8, axis=1)[..., None]
    return vals.transpose(0, 1, 3, 2).reshape(g * 512, n)


K, T, J, R, V, C, O, N, S = 512, 1024, 256, 512, 1024, 512, 128, 256, 1024


def setup_inputs():
    n = np.random.standard_normal
    idx = np.random.permutation(V)[:R]
    idx2 = np.random.permutation(T)[:J]
    idx3 = np.random.permutation(C)[:J]
    idx4 = np.random.permutation(C)[:C]
    idx5 = np.random.permutation(C)[:O]
    idx6 = np.random.permutation(J)[:O]
    idx7 = np.random.permutation(S)[:N]
    fk = mx_kscale(K)
    fr = mx_kscale(R)
    tr = np.ones(V)
    tr[idx] = fr
    xtp = pack_weight(n((K, T)) / fk[:, None], "e2m1")
    wtp = pack_weight(n((K, V)) * 1 / np.sqrt(K) * fk[:, None] * tr, "e5m2")
    w2p = pack_weight(n((K, R)) * 1 / np.sqrt(K) * fk[:, None], "e4m3")
    vsp = pack_weight(n((R, S)) * 1 / np.sqrt(R) / fr[:, None], "e4m3")
    return {
        "xt_words": xtp[0],
        "xt_scales": xtp[1],
        "wt_words": wtp[0],
        "wt_scales": wtp[1],
        "w2_words": w2p[0],
        "w2_scales": w2p[1],
        "vs_words": vsp[0],
        "vs_scales": vsp[1],
        "offs": striped(idx),
        "offs2": striped(idx2),
        "offs3": striped(idx3),
        "offs4": striped(idx4),
        "offs5": striped(idx5),
        "offs6": striped(idx6),
        "offs7": striped(idx7),
    }


def reference(xt_words, xt_scales, wt_words, wt_scales, w2_words, w2_scales, vs_words, vs_scales, offs, offs2, offs3, offs4, offs5, offs6, offs7):
    idx = unstriped(offs)
    idx2 = unstriped(offs2)
    idx3 = unstriped(offs3)
    idx4 = unstriped(offs4)
    idx5 = unstriped(offs5)
    idx6 = unstriped(offs6)
    idx7 = unstriped(offs7)
    xtu = unpack_weight(xt_words, xt_scales, "e2m1")
    wtu = unpack_weight(wt_words, wt_scales, "e5m2")
    w2u = unpack_weight(w2_words, w2_scales, "e4m3")
    vsu = unpack_weight(vs_words, vs_scales, "e4m3")
    wtidxg = wtu[:, idx]
    xtidx2g = xtu[:, idx2]
    a = wtidxg.T @ xtidx2g
    b = w2u.T @ xtidx2g
    lb = b[:, 0:1]
    la = a[:, 0:1]
    pw = np.zeros((R, C))
    pw[:, idx3] = a
    pg = np.maximum(pw, pw[:, idx4] * lb)
    hid = np.maximum(pg[:, idx5], b[:, idx6] * la)
    vsidx7g = vsu[:, idx7]
    hidq = mxq(hid, 0, "e5m2")
    y = vsidx7g.T @ hidq
    return y

@@ -1,0 +1,199 @@
+from contextlib import ExitStack
+
+import concourse.mybir as mybir
+
+K, T, J, R, V, C, O, N, S = 512, 1024, 256, 512, 1024, 512, 128, 256, 1024
+FLOPS = 2 * K * R * J * 2 + 2 * R * N * O
+
+F32 = mybir.dt.float32
+BF16 = mybir.dt.bfloat16
+I32 = mybir.dt.int32
+U32 = mybir.dt.uint32
+U16 = mybir.dt.uint16
+U8 = mybir.dt.uint8
+E4M3 = mybir.dt.float8_e4m3fn_x4
+E5M2 = mybir.dt.float8_e5m2_x4
+E2M1 = mybir.dt.float4_e2m1fn_x4
+COPY = mybir.ActivationFunctionType.Copy
+MAX = mybir.AluOpType.max
+
+P = 128
+PACK = 4
+QUADS = 4
+HALF = C // 2
+
+
+def tile_list_leadladder_storeleads_store_plain_kernel(
+    tc, xt_words, xt_scales, wt_words, wt_scales, w2_words, w2_scales, vs_words, vs_scales,
+    offs, offs2, offs3, offs4, offs5, offs6, offs7, out,
+):
+    nc = tc.nc
+    with ExitStack() as ctx:
+        sb = ctx.enter_context(tc.tile_pool(name="sb", bufs=1))
+        ps = ctx.enter_context(tc.psum_pool(name="ps", bufs=1))
+
+        def sbuf(name, cols, dtype):
+            return sb.tile([P, cols], dtype, name=name, align_bytes=64)
+
+        def load_list(name, src):
+            tile = sb.tile(list(src.shape), U16, name=name)
+            nc.sync.dma_start(tile[:], src)
+            return tile
+
+        def load_words(tile, src):
+            nc.sync.dma_start(tile[:].bitcast(I32), src.bitcast(I32))
+
+        def load_scale_rows(queue, tile, src):
+            rows = src[0].bitcast(I32)
+            for q in range(QUADS):
+                queue.dma_start(tile[32 * q : 32 * q + 4, :].bitcast(I32), rows[4 * q : 4 * q + 4, :])
+
+        def packed(words):
+            return words[0].rearrange("p n t -> p (n t)")
+
+        def dealt(ap):
+            return ap.rearrange("p (t q) -> p q t", t=PACK)
+
+        xt_w = sbuf("xt_w", T, U16)
+        xt_s = sbuf("xt_s", T, U8)
+        wt_w = sbuf("wt_w", V, U32)
+        wt_s = sbuf("wt_s", V, U8)
+        w2_w = sbuf("w2_w", R, U32)
+        w2_s = sbuf("w2_s", R, U8)
+        vs_w = sbuf("vs_w", S, U32)
+        vs_s = sbuf("vs_s", S, U8)
+        w2_rows = sb.tile([4, QUADS, R // 4], I32, name="w2_rows")
+        pw = [sbuf(f"pw{t}", C, F32) for t in range(PACK)]
+
+        for tile in (xt_s, wt_s, w2_s, vs_s):
+            nc.vector.memset(tile[:].bitcast(I32), 0)
+        for t in range(PACK):
+            nc.vector.memset(pw[t][:], 0.0)
+
+        l2 = load_list("l2", offs2)
+        load_scale_rows(nc.scalar, xt_s, xt_scales)
+        nc.sync.dma_start(w2_rows[:], w2_scales[0].bitcast(I32).rearrange("(q r) w -> r q w", r=4))
+        load_words(xt_w, xt_words[0])
+        load_words(wt_w, packed(wt_words))
+        l1 = load_list("l1", offs)
+        load_scale_rows(nc.sync, wt_s, wt_scales)
+        load_words(w2_w, packed(w2_words))
+        l3 = load_list("l3", offs3)
+        l7 = load_list("l7", offs7)
+        load_scale_rows(nc.sync, vs_s, vs_scales)
+        l4 = load_list("l4", offs4)
+        load_words(vs_w, packed(vs_words))
+        l6 = load_list("l6", offs6)
+        l5 = load_list("l5", offs5)
+
+        xg_s = sbuf("xg_s", J, U8)
+        xg_w = sbuf("xg_w", J, U16)
+        w2d_w = sbuf("w2d_w", R, U32)
+        w2d_s = sbuf("w2d_s", R, U8)
+        wg_s = sbuf("wg_s", R, U8)
+        wg_w = sbuf("wg_w", R, U32)
+        nc.vector.tensor_copy(xg_s[:], xt_s[:].indirect(l2[:]))
+        nc.vector.tensor_copy(xg_w[:], xt_w[:].indirect(l2[:]))
+        for q in range(QUADS):
+            nc.vector.tensor_copy(w2_s[32 * q : 32 * q + 4, :].bitcast(I32), w2_rows[:, q, :])
+        nc.vector.tensor_copy(dealt(w2d_s[:]), w2_s[:].rearrange("p (q t) -> p q t", t=PACK))
+        nc.scalar.copy(dealt(w2d_w[:]), w2_w[:].rearrange("p (q t) -> p q t", t=PACK))
+        nc.vector.tensor_copy(dealt(wg_w[:]), wt_w[:].indirect(l1[:]))
+        nc.vector.tensor_copy(dealt(wg_s[:]), wt_s[:].indirect(l1[:]))
+
+        def first_stage(acc, words, scales, fmt, t):
+            cols = slice(P * t, P * (t + 1))
+            nc.tensor.matmul_mx(
+                out=acc, lhsT=words[:, cols].bitcast(fmt), lhsT_scale=scales[:, cols],
+                rhs=xg_w[:].bitcast(E2M1), rhs_scale=xg_s[:], start=True, stop=True,
+            )
+
+        b_ps = [ps.tile([P, 2, J], F32, name=f"b_ps{h}") for h in range(2)]
+        b = [sbuf(f"b{t}", J, F32) for t in range(PACK)]
+        for t in range(PACK):
+            first_stage(b_ps[t // 2][:, t % 2, :], w2d_w, w2d_s, E4M3, t)
+        for t in range(PACK):
+            nc.scalar.copy(b[t][:], b_ps[t // 2][:, t % 2, :])
+
+        a0_ps = ps.tile([P, J], F32, name="a0_ps")
+        a1_ps = ps.tile([P, J], F32, name="a1_ps")
+        a23_ps = ps.tile([P, 2, J], F32, name="a23_ps")
+        a_ps = [a0_ps[:], a1_ps[:], a23_ps[:, 0, :], a23_ps[:, 1, :]]
+        for t in range(PACK):
+            first_stage(a_ps[t], wg_w, wg_s, E5M2, t)
+        a0 = sbuf("a0", J, F32)
+        a1 = sbuf("a1", J, F32)
+        a23 = sbuf("a23", 2 * J, F32)
+        a = [a0[:], a1[:], a23[:, 0:J], a23[:, J : 2 * J]]
+
+        kept = [sbuf(f"kept{t}", C, F32) for t in range(PACK)]
+        pg = [sbuf(f"pg{t}", C, F32) for t in range(PACK)]
+        g5 = sbuf("g5", PACK * O, F32)
+        g6 = sbuf("g6", PACK * O, F32)
+
+        def fetch_board(t):
+            for h in range(2):
+                cols = slice(HALF * h, HALF * (h + 1))
+                lst = l4[:, HALF // 16 * h : HALF // 16 * (h + 1)]
+                nc.scalar.activation(kept[t][:, cols], pw[t][:].indirect(lst), COPY, scale=b[t][:, 0:1])
+
+        def fetch_b(t):
+            nc.scalar.activation(g6[:, O * t : O * (t + 1)], b[t][:].indirect(l6[:]), COPY, scale=a[t][:, 0:1])
+
+        def keep(t, parts):
+            width = C // parts
+            for h in range(parts):
+                cols = slice(width * h, width * (h + 1))
+                nc.vector.tensor_tensor(pg[t][:, cols], pw[t][:, cols], kept[t][:, cols], MAX)
+
+        def pick(t, on_scalar):
+            if on_scalar:
+                nc.scalar.activation(g5[:, O * t : O * (t + 1)], pg[t][:].indirect(l5[:]), COPY)
+            else:
+                nc.vector.tensor_copy(g5[:, O * t : O * (t + 1)], pg[t][:].indirect(l5[:]))
+
+        vg_w = sbuf("vg_w", N, U32)
+        vg_s = sbuf("vg_s", N, U8)
+        nc.vector.tensor_copy(a0[:], a0_ps[:])
+        nc.scalar.copy(a1[:], a1_ps[:])
+        nc.scalar.copy(a23[:], a23_ps[:].rearrange("p h j -> p (h j)"))
+        nc.vector.tensor_copy(pw[0][:].indirect(l3[:]), a[0])
+        nc.scalar.activation(pw[1][:].indirect(l3[:]), a[1], COPY)
+        nc.vector.tensor_copy(pw[2][:].indirect(l3[:]), a[2])
+        nc.vector.tensor_copy(pw[3][:].indirect(l3[:]), a[3])
+        for t in range(PACK):
+            fetch_board(t)
+        for t in range(PACK):
+            fetch_b(t)
+        for t in range(PACK - 1):
+            keep(t, 1)
+        nc.vector.tensor_copy(vg_s[:], vs_s[:].indirect(l7[:]))
+        nc.vector.tensor_copy(vg_w[:], vs_w[:].indirect(l7[:]))
+        keep(PACK - 1, 1)
+        pick(0, True)
+        for t in range(1, PACK):
+            pick(t, False)
+
+        hid = sbuf("hid", O * PACK, BF16)
+        nc.vector.tensor_tensor(
+            hid[:].rearrange("p (c i t) -> p c t i", i=4, t=PACK),
+            g5[:].rearrange("p (t c i) -> p c t i", i=4, t=PACK),
+            g6[:].rearrange("p (t c i) -> p c t i", i=4, t=PACK),
+            MAX,
+        )
+        hq_w = sbuf("hq_w", O, U32)
+        hq_s = sbuf("hq_s", O, U8)
+        nc.vector.quantize_mx(out=hq_w[:].bitcast(E5M2), scales=hq_s[:], in_=hid[:])
+
+        y_ps = [ps.tile([P, O], F32, name=f"y_ps{h}") for h in range(2)]
+        y = [sbuf(f"y{h}", O, F32) for h in range(2)]
+        for h in range(2):
+            cols = slice(P * h, P * (h + 1))
+            nc.tensor.matmul_mx(
+                out=y_ps[h][:], lhsT=vg_w[:, cols].bitcast(E4M3), lhsT_scale=vg_s[:, cols],
+                rhs=hq_w[:].bitcast(E5M2), rhs_scale=hq_s[:], start=True, stop=True,
+            )
+        nc.vector.tensor_copy(y[0][:], y_ps[0][:])
+        nc.scalar.copy(y[1][:], y_ps[1][:])
+        nc.sync.dma_start(out[0:P, :], y[0][:])
+        nc.scalar.dma_start(out[P : 2 * P, :], y[1][:])

@@ -43,9 +43,9 @@ def tile_list_leadladder_storeleads_store_plain_kernel(
         def load_words(tile, src):
             nc.sync.dma_start(tile[:].bitcast(I32), src.bitcast(I32))
 
-        def load_scale_rows(queue, tile, src):
+        def load_scale_rows(queue, tile, src, quads=range(QUADS)):
             rows = src[0].bitcast(I32)
-            for q in range(QUADS):
+            for q in quads:
                 queue.dma_start(tile[32 * q : 32 * q + 4, :].bitcast(I32), rows[4 * q : 4 * q + 4, :])
 
         def packed(words):
@@ -62,27 +62,28 @@ def tile_list_leadladder_storeleads_store_plain_kernel(
         w2_s = sbuf("w2_s", R, U8)
         vs_w = sbuf("vs_w", S, U32)
         vs_s = sbuf("vs_s", S, U8)
-        w2_rows = sb.tile([4, QUADS, R // 4], I32, name="w2_rows")
-        pw = [sbuf(f"pw{t}", C, F32) for t in range(PACK)]
+        xt_rows = sb.tile([4, QUADS, T // 4], I32, name="xt_rows")
+        pw = [sbuf(f"pw{t}", 2 * C, F32) for t in range(PACK)]
 
-        for tile in (xt_s, wt_s, w2_s, vs_s):
+        for tile in (w2_s, wt_s, xt_s, vs_s):
             nc.vector.memset(tile[:].bitcast(I32), 0)
         for t in range(PACK):
-            nc.vector.memset(pw[t][:], 0.0)
+            nc.gpsimd.memset(pw[t][:, 0:C], 0.0)
 
         l2 = load_list("l2", offs2)
-        load_scale_rows(nc.scalar, xt_s, xt_scales)
-        nc.sync.dma_start(w2_rows[:], w2_scales[0].bitcast(I32).rearrange("(q r) w -> r q w", r=4))
+        load_scale_rows(nc.scalar, w2_s, w2_scales, range(0, 2))
+        nc.sync.dma_start(xt_rows[:], xt_scales[0].bitcast(I32).rearrange("(q r) w -> r q w", r=4))
         load_words(xt_w, xt_words[0])
-        load_words(wt_w, packed(wt_words))
         l1 = load_list("l1", offs)
-        load_scale_rows(nc.sync, wt_s, wt_scales)
+        load_words(wt_w, packed(wt_words))
         load_words(w2_w, packed(w2_words))
-        l3 = load_list("l3", offs3)
+        load_scale_rows(nc.sync, w2_s, w2_scales, range(2, 4))
+        load_scale_rows(nc.sync, wt_s, wt_scales)
+        load_words(vs_w, packed(vs_words))
         l7 = load_list("l7", offs7)
         load_scale_rows(nc.sync, vs_s, vs_scales)
+        l3 = load_list("l3", offs3)
         l4 = load_list("l4", offs4)
-        load_words(vs_w, packed(vs_words))
         l6 = load_list("l6", offs6)
         l5 = load_list("l5", offs5)
 
@@ -92,11 +93,11 @@ def tile_list_leadladder_storeleads_store_plain_kernel(
         w2d_s = sbuf("w2d_s", R, U8)
         wg_s = sbuf("wg_s", R, U8)
         wg_w = sbuf("wg_w", R, U32)
+        for q in range(QUADS):
+            nc.vector.tensor_copy(xt_s[32 * q : 32 * q + 4, :].bitcast(I32), xt_rows[:, q, :])
         nc.vector.tensor_copy(xg_s[:], xt_s[:].indirect(l2[:]))
         nc.vector.tensor_copy(xg_w[:], xt_w[:].indirect(l2[:]))
-        for q in range(QUADS):
-            nc.vector.tensor_copy(w2_s[32 * q : 32 * q + 4, :].bitcast(I32), w2_rows[:, q, :])
-        nc.vector.tensor_copy(dealt(w2d_s[:]), w2_s[:].rearrange("p (q t) -> p q t", t=PACK))
+        nc.gpsimd.tensor_copy(w2d_s[:].rearrange("p (t q) -> p t q", t=PACK), w2_s[:].rearrange("p (q t) -> p t q", t=PACK))
         nc.scalar.copy(dealt(w2d_w[:]), w2_w[:].rearrange("p (q t) -> p q t", t=PACK))
         nc.vector.tensor_copy(dealt(wg_w[:]), wt_w[:].indirect(l1[:]))
         nc.vector.tensor_copy(dealt(wg_s[:]), wt_s[:].indirect(l1[:]))
@@ -132,10 +133,7 @@ def tile_list_leadladder_storeleads_store_plain_kernel(
         g6 = sbuf("g6", PACK * O, F32)
 
         def fetch_board(t):
-            for h in range(2):
-                cols = slice(HALF * h, HALF * (h + 1))
-                lst = l4[:, HALF // 16 * h : HALF // 16 * (h + 1)]
-                nc.scalar.activation(kept[t][:, cols], pw[t][:].indirect(lst), COPY, scale=b[t][:, 0:1])
+            nc.scalar.activation(kept[t][:], pw[t][:].indirect(l4[:]), COPY, scale=b[t][:, 0:1])
 
         def fetch_b(t):
             nc.scalar.activation(g6[:, O * t : O * (t + 1)], b[t][:].indirect(l6[:]), COPY, scale=a[t][:, 0:1])
@@ -154,7 +152,9 @@ def tile_list_leadladder_storeleads_store_plain_kernel(
 
         vg_w = sbuf("vg_w", N, U32)
         vg_s = sbuf("vg_s", N, U8)
-        nc.vector.tensor_copy(a0[:], a0_ps[:])
+        nc.vector.tensor_copy(vg_s[:], vs_s[:].indirect(l7[:]))
+        nc.vector.tensor_copy(vg_w[:], vs_w[:].indirect(l7[:]))
+        nc.scalar.copy(a0[:], a0_ps[:])
         nc.scalar.copy(a1[:], a1_ps[:])
         nc.scalar.copy(a23[:], a23_ps[:].rearrange("p h j -> p (h j)"))
         nc.vector.tensor_copy(pw[0][:].indirect(l3[:]), a[0])
@@ -167,20 +167,20 @@ def tile_list_leadladder_storeleads_store_plain_kernel(
             fetch_b(t)
         for t in range(PACK - 1):
             keep(t, 1)
-        nc.vector.tensor_copy(vg_s[:], vs_s[:].indirect(l7[:]))
-        nc.vector.tensor_copy(vg_w[:], vs_w[:].indirect(l7[:]))
         keep(PACK - 1, 1)
-        pick(0, True)
+        pick(0, False)
         for t in range(1, PACK):
             pick(t, False)
 
         hid = sbuf("hid", O * PACK, BF16)
-        nc.vector.tensor_tensor(
-            hid[:].rearrange("p (c i t) -> p c t i", i=4, t=PACK),
-            g5[:].rearrange("p (t c i) -> p c t i", i=4, t=PACK),
-            g6[:].rearrange("p (t c i) -> p c t i", i=4, t=PACK),
-            MAX,
-        )
+        for h in range(2):
+            pair = slice(2 * h, 2 * h + 2)
+            nc.vector.tensor_tensor(
+                hid[:].rearrange("p (o t) -> p o t", t=PACK)[:, :, pair],
+                g5[:].rearrange("p (t o) -> p o t", t=PACK)[:, :, pair],
+                g6[:].rearrange("p (t o) -> p o t", t=PACK)[:, :, pair],
+                MAX,
+            )
         hq_w = sbuf("hq_w", O, U32)
         hq_s = sbuf("hq_s", O, U8)
         nc.vector.quantize_mx(out=hq_w[:].bitcast(E5M2), scales=hq_s[:], in_=hid[:])

from contextlib import ExitStack

import concourse.mybir as mybir

K, T, J, R, V, C, O, N, S = 512, 1024, 256, 512, 1024, 512, 128, 256, 1024
FLOPS = 2 * K * R * J * 2 + 2 * R * N * O

F32 = mybir.dt.float32
BF16 = mybir.dt.bfloat16
I32 = mybir.dt.int32
U32 = mybir.dt.uint32
U16 = mybir.dt.uint16
U8 = mybir.dt.uint8
E4M3 = mybir.dt.float8_e4m3fn_x4
E5M2 = mybir.dt.float8_e5m2_x4
E2M1 = mybir.dt.float4_e2m1fn_x4
COPY = mybir.ActivationFunctionType.Copy
MAX = mybir.AluOpType.max

P = 128
PACK = 4
QUADS = 4
HALF = C // 2


def tile_list_leadladder_storeleads_store_plain_kernel(
    tc, xt_words, xt_scales, wt_words, wt_scales, w2_words, w2_scales, vs_words, vs_scales,
    offs, offs2, offs3, offs4, offs5, offs6, offs7, out,
):
    nc = tc.nc
    with ExitStack() as ctx:
        sb = ctx.enter_context(tc.tile_pool(name="sb", bufs=1))
        ps = ctx.enter_context(tc.psum_pool(name="ps", bufs=1))

        def sbuf(name, cols, dtype):
            return sb.tile([P, cols], dtype, name=name, align_bytes=64)

        def load_list(name, src):
            tile = sb.tile(list(src.shape), U16, name=name)
            nc.sync.dma_start(tile[:], src)
            return tile

        def load_words(tile, src):
            nc.sync.dma_start(tile[:].bitcast(I32), src.bitcast(I32))

        def load_scale_rows(queue, tile, src, quads=range(QUADS)):
            rows = src[0].bitcast(I32)
            for q in quads:
                queue.dma_start(tile[32 * q : 32 * q + 4, :].bitcast(I32), rows[4 * q : 4 * q + 4, :])

        def packed(words):
            return words[0].rearrange("p n t -> p (n t)")

        def dealt(ap):
            return ap.rearrange("p (t q) -> p q t", t=PACK)

        xt_w = sbuf("xt_w", T, U16)
        xt_s = sbuf("xt_s", T, U8)
        wt_w = sbuf("wt_w", V, U32)
        wt_s = sbuf("wt_s", V, U8)
        w2_w = sbuf("w2_w", R, U32)
        w2_s = sbuf("w2_s", R, U8)
        vs_w = sbuf("vs_w", S, U32)
        vs_s = sbuf("vs_s", S, U8)
        xt_rows = sb.tile([4, QUADS, T // 4], I32, name="xt_rows")
        pw = [sbuf(f"pw{t}", 2 * C, F32) for t in range(PACK)]

        for tile in (w2_s, wt_s, xt_s, vs_s):
            nc.vector.memset(tile[:].bitcast(I32), 0)
        for t in range(PACK):
            nc.gpsimd.memset(pw[t][:, 0:C], 0.0)

        l2 = load_list("l2", offs2)
        load_scale_rows(nc.scalar, w2_s, w2_scales, range(0, 2))
        nc.sync.dma_start(xt_rows[:], xt_scales[0].bitcast(I32).rearrange("(q r) w -> r q w", r=4))
        load_words(xt_w, xt_words[0])
        l1 = load_list("l1", offs)
        load_words(wt_w, packed(wt_words))
        load_words(w2_w, packed(w2_words))
        load_scale_rows(nc.sync, w2_s, w2_scales, range(2, 4))
        load_scale_rows(nc.sync, wt_s, wt_scales)
        load_words(vs_w, packed(vs_words))
        l7 = load_list("l7", offs7)
        load_scale_rows(nc.sync, vs_s, vs_scales)
        l3 = load_list("l3", offs3)
        l4 = load_list("l4", offs4)
        l6 = load_list("l6", offs6)
        l5 = load_list("l5", offs5)

        xg_s = sbuf("xg_s", J, U8)
        xg_w = sbuf("xg_w", J, U16)
        w2d_w = sbuf("w2d_w", R, U32)
        w2d_s = sbuf("w2d_s", R, U8)
        wg_s = sbuf("wg_s", R, U8)
        wg_w = sbuf("wg_w", R, U32)
        for q in range(QUADS):
            nc.vector.tensor_copy(xt_s[32 * q : 32 * q + 4, :].bitcast(I32), xt_rows[:, q, :])
        nc.vector.tensor_copy(xg_s[:], xt_s[:].indirect(l2[:]))
        nc.vector.tensor_copy(xg_w[:], xt_w[:].indirect(l2[:]))
        nc.gpsimd.tensor_copy(w2d_s[:].rearrange("p (t q) -> p t q", t=PACK), w2_s[:].rearrange("p (q t) -> p t q", t=PACK))
        nc.scalar.copy(dealt(w2d_w[:]), w2_w[:].rearrange("p (q t) -> p q t", t=PACK))
        nc.vector.tensor_copy(dealt(wg_w[:]), wt_w[:].indirect(l1[:]))
        nc.vector.tensor_copy(dealt(wg_s[:]), wt_s[:].indirect(l1[:]))

        def first_stage(acc, words, scales, fmt, t):
            cols = slice(P * t, P * (t + 1))
            nc.tensor.matmul_mx(
                out=acc, lhsT=words[:, cols].bitcast(fmt), lhsT_scale=scales[:, cols],
                rhs=xg_w[:].bitcast(E2M1), rhs_scale=xg_s[:], start=True, stop=True,
            )

        b_ps = [ps.tile([P, 2, J], F32, name=f"b_ps{h}") for h in range(2)]
        b = [sbuf(f"b{t}", J, F32) for t in range(PACK)]
        for t in range(PACK):
            first_stage(b_ps[t // 2][:, t % 2, :], w2d_w, w2d_s, E4M3, t)
        for t in range(PACK):
            nc.scalar.copy(b[t][:], b_ps[t // 2][:, t % 2, :])

        a0_ps = ps.tile([P, J], F32, name="a0_ps")
        a1_ps = ps.tile([P, J], F32, name="a1_ps")
        a23_ps = ps.tile([P, 2, J], F32, name="a23_ps")
        a_ps = [a0_ps[:], a1_ps[:], a23_ps[:, 0, :], a23_ps[:, 1, :]]
        for t in range(PACK):
            first_stage(a_ps[t], wg_w, wg_s, E5M2, t)
        a0 = sbuf("a0", J, F32)
        a1 = sbuf("a1", J, F32)
        a23 = sbuf("a23", 2 * J, F32)
        a = [a0[:], a1[:], a23[:, 0:J], a23[:, J : 2 * J]]

        kept = [sbuf(f"kept{t}", C, F32) for t in range(PACK)]
        pg = [sbuf(f"pg{t}", C, F32) for t in range(PACK)]
        g5 = sbuf("g5", PACK * O, F32)
        g6 = sbuf("g6", PACK * O, F32)

        def fetch_board(t):
            nc.scalar.activation(kept[t][:], pw[t][:].indirect(l4[:]), COPY, scale=b[t][:, 0:1])

        def fetch_b(t):
            nc.scalar.activation(g6[:, O * t : O * (t + 1)], b[t][:].indirect(l6[:]), COPY, scale=a[t][:, 0:1])

        def keep(t, parts):
            width = C // parts
            for h in range(parts):
                cols = slice(width * h, width * (h + 1))
                nc.vector.tensor_tensor(pg[t][:, cols], pw[t][:, cols], kept[t][:, cols], MAX)

        def pick(t, on_scalar):
            if on_scalar:
                nc.scalar.activation(g5[:, O * t : O * (t + 1)], pg[t][:].indirect(l5[:]), COPY)
            else:
                nc.vector.tensor_copy(g5[:, O * t : O * (t + 1)], pg[t][:].indirect(l5[:]))

        vg_w = sbuf("vg_w", N, U32)
        vg_s = sbuf("vg_s", N, U8)
        nc.vector.tensor_copy(vg_s[:], vs_s[:].indirect(l7[:]))
        nc.vector.tensor_copy(vg_w[:], vs_w[:].indirect(l7[:]))
        nc.scalar.copy(a0[:], a0_ps[:])
        nc.scalar.copy(a1[:], a1_ps[:])
        nc.scalar.copy(a23[:], a23_ps[:].rearrange("p h j -> p (h j)"))
        nc.vector.tensor_copy(pw[0][:].indirect(l3[:]), a[0])
        nc.scalar.activation(pw[1][:].indirect(l3[:]), a[1], COPY)
        nc.vector.tensor_copy(pw[2][:].indirect(l3[:]), a[2])
        nc.vector.tensor_copy(pw[3][:].indirect(l3[:]), a[3])
        for t in range(PACK):
            fetch_board(t)
        for t in range(PACK):
            fetch_b(t)
        for t in range(PACK - 1):
            keep(t, 1)
        keep(PACK - 1, 1)
        pick(0, False)
        for t in range(1, PACK):
            pick(t, False)

        hid = sbuf("hid", O * PACK, BF16)
        for h in range(2):
            pair = slice(2 * h, 2 * h + 2)
            nc.vector.tensor_tensor(
                hid[:].rearrange("p (o t) -> p o t", t=PACK)[:, :, pair],
                g5[:].rearrange("p (t o) -> p o t", t=PACK)[:, :, pair],
                g6[:].rearrange("p (t o) -> p o t", t=PACK)[:, :, pair],
                MAX,
            )
        hq_w = sbuf("hq_w", O, U32)
        hq_s = sbuf("hq_s", O, U8)
        nc.vector.quantize_mx(out=hq_w[:].bitcast(E5M2), scales=hq_s[:], in_=hid[:])

        y_ps = [ps.tile([P, O], F32, name=f"y_ps{h}") for h in range(2)]
        y = [sbuf(f"y{h}", O, F32) for h in range(2)]
        for h in range(2):
            cols = slice(P * h, P * (h + 1))
            nc.tensor.matmul_mx(
                out=y_ps[h][:], lhsT=vg_w[:, cols].bitcast(E4M3), lhsT_scale=vg_s[:, cols],
                rhs=hq_w[:].bitcast(E5M2), rhs_scale=hq_s[:], start=True, stop=True,
            )
        nc.vector.tensor_copy(y[0][:], y_ps[0][:])
        nc.scalar.copy(y[1][:], y_ps[1][:])
        nc.sync.dma_start(out[0:P, :], y[0][:])
        nc.scalar.dma_start(out[P : 2 * P, :], y[1][:])
